import numpy as np
CORES = [1,2,5,6,25,26,29,30]
N = 8
ROOT = 7
WIDTHS = [1,2,2,0,0,0,4,2]
OFF = [0,1,3,5,5,5,5,9]
C = 11
def setup_inputs(rng):
    return {"x": rng.standard_normal((N, 128, C), dtype=np.float32)}
def reference(x):
    YW = max(WIDTHS)
    y = np.full((N, 128, YW), np.nan, x.dtype)
    for r in range(N):
        y[r][:, :WIDTHS[r]] = x[ROOT][:, OFF[r]:OFF[r] + WIDTHS[r]]
    return {"y": y}

@@ -1,0 +1,47 @@
+import comms_topo
+
+SCRATCH = {
+    "stage": ("sbuf", [128, 11], "float32"),
+    "land": ("sbuf", [128, 4], "float32"),
+}
+SEMAPHORES = ["loaded", "sent", "arrived", "stored"]
+
+OFF_CHIP = 0x00FF
+ON_CHIP = 0xFF00
+ENGINES = 8
+
+
+def rank_program(g, core, T, topo):
+    rank = T.rank_of(core)
+    if rank is None:
+        return
+    widths, off = T.tables["WIDTHS"], T.tables["OFF"]
+    root = T.root
+    w = widths[rank]
+
+    if rank != root:
+        if w == 0:
+            return
+        g.wait_ge(T.sem.arrived, ENGINES)
+        g.dma_start(T.y[:, 0:w], T.land[:, 0:w], allow_slow_non_contiguous=(w == 1)).then_inc(T.sem.stored, 16)
+        g.wait_ge(T.sem.stored, 16)
+        return
+
+    if w:
+        g.scalar.dma_start(T.y[:, 0:w], T.x[:, off[rank]:off[rank] + w]).then_inc(T.sem.stored, 16)
+    others = [r for r in range(len(T.cores)) if r != root and widths[r]]
+    lo = min(off[r] for r in others)
+    hi = max(off[r] + widths[r] for r in others)
+    g.sync.dma_start(T.stage[:, lo:hi], T.x[:, lo:hi]).then_inc(T.sem.loaded, 16)
+    g.wait_ge(T.sem.loaded, 16)
+    for r in others:
+        dst = T.cores[r]
+        rid, pid, _se = topo.addr(dst)
+        g.remote_dma(
+            T.land[:, 0:widths[r]], T.stage[:, off[r]:off[r] + widths[r]],
+            remote_sem=T.sem.arrived, local_sem=T.sem.sent, pid=pid, routing_id=rid,
+            dma_engine_mask=ON_CHIP if topo.chip(dst) == topo.chip(core) else OFF_CHIP,
+        )
+    g.wait_ge(T.sem.sent, ENGINES * len(others))
+    if w:
+        g.wait_ge(T.sem.stored, 16)

@@ -1,47 +1,78 @@
-import comms_topo
+from concourse.bass import DstId, RemoteDMATransfer
 
+WIDTHS = [1, 2, 2, 0, 0, 0, 4, 2]
+ROOT = 7
 SCRATCH = {
-    "stage": ("sbuf", [128, 11], "float32"),
-    "land": ("sbuf", [128, 4], "float32"),
+    "piece%d" % r: ("dram", [128, w], "float32") for r, w in enumerate(WIDTHS) if w and r != ROOT
 }
-SEMAPHORES = ["loaded", "sent", "arrived", "stored"]
+SEMAPHORES = ["packed%d" % r for r in range(len(WIDTHS))] + ["sent", "arrived", "stored"]
 
-OFF_CHIP = 0x00FF
-ON_CHIP = 0xFF00
-ENGINES = 8
+
+def engines_of(w):
+    n = 1
+    while n * 2 <= min(w, 8):
+        n *= 2
+    return n
 
 
 def rank_program(g, core, T, topo):
     rank = T.rank_of(core)
     if rank is None:
         return
-    widths, off = T.tables["WIDTHS"], T.tables["OFF"]
-    root = T.root
+    widths, off, root = T.tables["WIDTHS"], T.tables["OFF"], T.root
+    if list(widths) != WIDTHS or root != ROOT:
+        raise ValueError("SCRATCH was laid out for other widths")
     w = widths[rank]
+
+    def local_copy(q, out, in_, width, sem):
+        if width == 1:
+            g.dma_start(out, in_, allow_slow_non_contiguous=True).then_inc(sem, 16)
+        else:
+            q.dma_start(out, in_).then_inc(sem, 16)
 
     if rank != root:
         if w == 0:
             return
-        g.wait_ge(T.sem.arrived, ENGINES)
-        g.dma_start(T.y[:, 0:w], T.land[:, 0:w], allow_slow_non_contiguous=(w == 1)).then_inc(T.sem.stored, 16)
-        g.wait_ge(T.sem.stored, 16)
+        q = g if w == 1 else g.sync
+        q.wait_ge(T.sem.arrived, engines_of(w))
+        local_copy(q, T.y[:, 0:w], T["piece%d" % rank][:, :], w, T.sem.stored)
+        q.wait_ge(T.sem.stored, 16)
         return
 
+    def on_chip(r):
+        return topo.chip(T.cores[r]) == topo.chip(core)
+
+    others = sorted((r for r in range(len(T.cores)) if r != root and widths[r]), key=on_chip)
+
+    hw = [g.sync, g.scalar]
+    for i, r in enumerate(others):
+        local_copy(hw[i % 2], T["piece%d" % r][:, :], T.x[:, off[r]:off[r] + widths[r]], widths[r],
+                   T.sem["packed%d" % r])
     if w:
-        g.scalar.dma_start(T.y[:, 0:w], T.x[:, off[rank]:off[rank] + w]).then_inc(T.sem.stored, 16)
-    others = [r for r in range(len(T.cores)) if r != root and widths[r]]
-    lo = min(off[r] for r in others)
-    hi = max(off[r] + widths[r] for r in others)
-    g.sync.dma_start(T.stage[:, lo:hi], T.x[:, lo:hi]).then_inc(T.sem.loaded, 16)
-    g.wait_ge(T.sem.loaded, 16)
+        local_copy(hw[len(others) % 2], T.y[:, 0:w], T.x[:, off[rank]:off[rank] + w], w, T.sem.stored)
+
+    used = {False: 0, True: 0}
+    total = 0
+    call_widths = []
     for r in others:
-        dst = T.cores[r]
-        rid, pid, _se = topo.addr(dst)
-        g.remote_dma(
-            T.land[:, 0:widths[r]], T.stage[:, off[r]:off[r] + widths[r]],
-            remote_sem=T.sem.arrived, local_sem=T.sem.sent, pid=pid, routing_id=rid,
-            dma_engine_mask=ON_CHIP if topo.chip(dst) == topo.chip(core) else OFF_CHIP,
-        )
-    g.wait_ge(T.sem.sent, ENGINES * len(others))
+        if widths[r] not in call_widths:
+            call_widths.append(widths[r])
+    for width in call_widths:
+        n = engines_of(width)
+        transfers = []
+        for r in (r for r in others if widths[r] == width):
+            here = on_chip(r)
+            if used[here] + n > 8:
+                raise ValueError("more pieces than engines: the masks would overlap")
+            mask = ((1 << n) - 1) << (used[here] + (8 if here else 0))
+            used[here] += n
+            total += n
+            rid, pid, _se = topo.addr(T.cores[r])
+            g.wait_ge(T.sem["packed%d" % r], 16)
+            transfers.append(RemoteDMATransfer(
+                dst_ids=[DstId(rid=rid, pnc=pid)], dma_engine_mask=mask, remote_sem=T.sem.arrived,
+                src=T["piece%d" % r][:, :], dst=T["piece%d" % r][:, :]))
+        g.remote_dma_fused(transfers, local_sem=T.sem.sent)
+    g.wait_ge(T.sem.sent, total)
     if w:
         g.wait_ge(T.sem.stored, 16)

from concourse.bass import DstId, RemoteDMATransfer

WIDTHS = [1, 2, 2, 0, 0, 0, 4, 2]
ROOT = 7
SCRATCH = {
    "piece%d" % r: ("dram", [128, w], "float32") for r, w in enumerate(WIDTHS) if w and r != ROOT
}
SEMAPHORES = ["packed%d" % r for r in range(len(WIDTHS))] + ["sent", "arrived", "stored"]


def engines_of(w):
    n = 1
    while n * 2 <= min(w, 8):
        n *= 2
    return n


def rank_program(g, core, T, topo):
    rank = T.rank_of(core)
    if rank is None:
        return
    widths, off, root = T.tables["WIDTHS"], T.tables["OFF"], T.root
    if list(widths) != WIDTHS or root != ROOT:
        raise ValueError("SCRATCH was laid out for other widths")
    w = widths[rank]

    def local_copy(q, out, in_, width, sem):
        if width == 1:
            g.dma_start(out, in_, allow_slow_non_contiguous=True).then_inc(sem, 16)
        else:
            q.dma_start(out, in_).then_inc(sem, 16)

    if rank != root:
        if w == 0:
            return
        q = g if w == 1 else g.sync
        q.wait_ge(T.sem.arrived, engines_of(w))
        local_copy(q, T.y[:, 0:w], T["piece%d" % rank][:, :], w, T.sem.stored)
        q.wait_ge(T.sem.stored, 16)
        return

    def on_chip(r):
        return topo.chip(T.cores[r]) == topo.chip(core)

    others = sorted((r for r in range(len(T.cores)) if r != root and widths[r]), key=on_chip)

    hw = [g.sync, g.scalar]
    for i, r in enumerate(others):
        local_copy(hw[i % 2], T["piece%d" % r][:, :], T.x[:, off[r]:off[r] + widths[r]], widths[r],
                   T.sem["packed%d" % r])
    if w:
        local_copy(hw[len(others) % 2], T.y[:, 0:w], T.x[:, off[rank]:off[rank] + w], w, T.sem.stored)

    used = {False: 0, True: 0}
    total = 0
    call_widths = []
    for r in others:
        if widths[r] not in call_widths:
            call_widths.append(widths[r])
    for width in call_widths:
        n = engines_of(width)
        transfers = []
        for r in (r for r in others if widths[r] == width):
            here = on_chip(r)
            if used[here] + n > 8:
                raise ValueError("more pieces than engines: the masks would overlap")
            mask = ((1 << n) - 1) << (used[here] + (8 if here else 0))
            used[here] += n
            total += n
            rid, pid, _se = topo.addr(T.cores[r])
            g.wait_ge(T.sem["packed%d" % r], 16)
            transfers.append(RemoteDMATransfer(
                dst_ids=[DstId(rid=rid, pnc=pid)], dma_engine_mask=mask, remote_sem=T.sem.arrived,
                src=T["piece%d" % r][:, :], dst=T["piece%d" % r][:, :]))
        g.remote_dma_fused(transfers, local_sem=T.sem.sent)
    g.wait_ge(T.sem.sent, total)
    if w:
        g.wait_ge(T.sem.stored, 16)
